import numpy as np
import ml_dtypes


def mxq(x, axis, fmt="e4m3"):
    dtype, down = {"e4m3": (ml_dtypes.float8_e4m3fn, 7), "e5m2": (ml_dtypes.float8_e5m2, 14)}[fmt]
    v = np.moveaxis(np.asarray(x, np.float32).astype(ml_dtypes.bfloat16).astype(np.float64), axis, -1)
    blocks = v.reshape(v.shape[:-1] + (-1, 32))
    amax = np.abs(blocks).max(-1, keepdims=True)
    byte = np.maximum(np.where(amax > 0, np.frexp(amax)[1] - 1 + 127, 0) - down, 1)
    scale = np.exp2(byte - 127.0)
    codes = (blocks / scale).astype(np.float32).astype(dtype).astype(np.float64)
    return np.moveaxis((codes * scale).reshape(v.shape), -1, axis)


WIDE = False


def mx_kscale(k):
    if not WIDE:
        return np.ones(k)
    levels = np.array([10, -10, 5, -5, 0])
    if k % 512:
        return np.exp2(np.random.permutation(np.resize(levels, k // 32))).repeat(32)
    a = np.empty((k // 512, 16))
    for p in range(k // 512):
        a[p, :8] = np.random.permutation(np.resize(levels, 8))
        for g in range(8):
            far = levels[np.abs(levels - a[p, g]) >= 10]
            a[p, g + 8] = far[np.random.randint(len(far))]
    return np.exp2(a.ravel()).repeat(32)


def f64(x):
    return np.asarray(x).astype(np.float64)


E2M1 = np.array([0.0, 0.5, 1.0, 1.5, 2.0, 3.0, 4.0, 6.0, -0.0, -0.5, -1.0, -1.5, -2.0, -3.0, -4.0, -6.0])


def pack_weight(w, fmt):
    k, n = w.shape
    w = f64(np.asarray(w, np.float32).astype(ml_dtypes.bfloat16)).reshape(k // 32, 32, n)
    amax = np.abs(w).max(1)
    if fmt == "e4m3":
        byte = np.frexp(amax)[1] - 1 + 127 - 7
    else:
        mant, ex = np.frexp(amax / 6.0)
        byte = np.where(mant > 0.5, ex, ex - 1) + 127
    byte = np.clip(np.where(amax > 0, byte, 1), 1, 254)
    scaled = (w * np.exp2(127.0 - byte)[:, None, :]).reshape(k, n).astype(np.float32)
    by_word = np.ascontiguousarray(scaled.reshape(k // 512, 128, 4, n).transpose(0, 1, 3, 2))
    if fmt == "e4m3":
        words = by_word.astype(ml_dtypes.float8_e4m3fn).view(np.uint8)
    else:
        c = by_word.astype(ml_dtypes.float4_e2m1fn).view(np.uint8) & 0xF
        words = (c[..., 0::2] | (c[..., 1::2] << 4)).reshape(k // 512, 128, 2 * n)
    return np.ascontiguousarray(words), np.ascontiguousarray(byte.astype(np.uint8).reshape(k // 512, 16, n))


def unpack_weight(words, scales, fmt):
    g, _, n = scales.shape
    words = np.ascontiguousarray(words).reshape(g, 128, n, -1)
    if fmt == "e4m3":
        vals = words.view(ml_dtypes.float8_e4m3fn).astype(np.float64)
    else:
        nib = np.empty((g, 128, n, 4), np.uint8)
        nib[..., 0::2] = words & 0xF
        nib[..., 1::2] = words >> 4
        vals = E2M1[nib]
    vals = vals * np.repeat(np.exp2(scales.astype(np.float64) - 127.0), 8, axis=1)[..., None]
    return vals.transpose(0, 1, 3, 2).reshape(g * 512, n)


K, L, T, N = 1024, 512, 512, 512


def setup_inputs():
    n = np.random.standard_normal
    fk = mx_kscale(K)
    fl = mx_kscale(L)
    xtp = pack_weight(n((K, T)) * np.random.uniform(0.3, 1.7, (1, T)) / fk[:, None], "e4m3")
    xsp = pack_weight(n((L, T)) / fl[:, None], "e2m1")
    wsp = pack_weight(n((L, N)) * 1 / np.sqrt(L) * fl[:, None], "e4m3")
    wcp = pack_weight(n((K, N)) * 1 / np.sqrt(K) * fk[:, None], "e2m1")
    return {
        "xt_words": xtp[0],
        "xt_scales": xtp[1],
        "wa": (n((K, N)) * 1 / np.sqrt(K) * fk[:, None]).astype(np.float32),
        "xs_words": xsp[0],
        "xs_scales": xsp[1],
        "ws_words": wsp[0],
        "ws_scales": wsp[1],
        "wc_words": wcp[0],
        "wc_scales": wcp[1],
        "bi": (np.random.uniform(-0.8, 0.8, (1, N))).astype(np.float32),
    }


def reference(xt_words, xt_scales, wa, xs_words, xs_scales, ws_words, ws_scales, wc_words, wc_scales, bi):
    xtu = unpack_weight(xt_words, xt_scales, "e4m3")
    xsu = unpack_weight(xs_words, xs_scales, "e2m1")
    wsu = unpack_weight(ws_words, ws_scales, "e4m3")
    wcu = unpack_weight(wc_words, wc_scales, "e2m1")
    waq = mxq(f64(wa), 0, "e4m3")
    a0 = xtu.T @ waq + xsu.T @ wsu
    b0 = xtu.T @ wcu
    a = a0 + f64(bi)
    b = b0 + f64(bi)
    s = np.tanh(2.0 * np.mean(a * b, axis=1, keepdims=True))
    y = a + s * b
    return y

@@ -1,0 +1,241 @@
+from contextlib import ExitStack
+
+import concourse.mybir as mybir
+from concourse.masks import make_identity
+
+K, L, T, N = 1024, 512, 512, 512
+FLOPS = 2 * T * N * (2 * K + L)
+
+F32 = mybir.dt.float32
+BF16 = mybir.dt.bfloat16
+I32 = mybir.dt.int32
+U8 = mybir.dt.uint8
+FP8X4 = mybir.dt.float8_e4m3fn_x4
+FP4X4 = mybir.dt.float4_e2m1fn_x4
+ALU = mybir.AluOpType
+ACT = mybir.ActivationFunctionType
+
+P = 128
+HALF = 256
+
+
+def tile_mix_rows_heard_by_agreement_kernel(
+    tc, xt_words, xt_scales, wa, xs_words, xs_scales, ws_words, ws_scales, wc_words, wc_scales, bi, out
+):
+    nc = tc.nc
+    with ExitStack() as ctx:
+        sb = ctx.enter_context(tc.tile_pool(name="sb", bufs=1))
+        ps = ctx.enter_context(tc.psum_pool(name="ps", bufs=1))
+        ctx.enter_context(tc.manual_schedule())
+
+        def tile(name, shape, dtype):
+            return sb.tile(shape, dtype, name=name, tag=name, align_bytes=64)
+
+        xt_w = tile("xt_w", [P, 2, T], I32)
+        xt_s = tile("xt_s", [P, 2, T], U8)
+        wc_w = tile("wc_w", [P, 2, 2 * N], U8)
+        wc_s = tile("wc_s", [P, 2, N], U8)
+        xs_w = tile("xs_w", [P, 2 * T], U8)
+        xs_s = tile("xs_s", [P, 1, T], U8)
+        ws_w = tile("ws_w", [P, N], I32)
+        ws_s = tile("ws_s", [P, 1, N], U8)
+        bias_col = tile("bias_col", [P, 4], F32)
+        bias_row = tile("bias_row", [P, N], F32)
+        ident = tile("ident", [P, P], F32)
+        warm_in = tile("warm_in", [P, 1], F32)
+        warm_out = tile("warm_out", [P, 1], F32)
+        keys = [(h, z) for h in range(2) for z in range(2)]
+        raw = {k: tile("raw%d%d" % k, [P, 4, HALF], F32) for k in keys}
+        grp = {k: tile("grp%d%d" % k, [P, HALF, 4], BF16) for k in keys}
+        wa_w = {k: tile("wa_w%d%d" % k, [P, HALF], I32) for k in keys}
+        wa_s = {k: tile("wa_s%d%d" % k, [P, HALF], U8) for k in keys}
+        b_sb = [tile("b_sb%d" % t, [P, N], F32) for t in range(4)]
+        at_sb = [tile("at_sb%d" % j, [P, T], F32) for j in range(4)]
+        y_sb = [tile("y_sb%d" % t, [P, N], F32) for t in range(4)]
+        prod = [tile("prod%d" % i, [P, HALF], F32) for i in range(2)]
+        part = [tile("part%d" % h, [P, 4], F32) for h in range(2)]
+        gate = tile("gate", [P, 4], F32)
+
+        def cols(i, width=P):
+            return slice(i * width, (i + 1) * width)
+
+        def load_scales(engine, plane, scales, q):
+            engine.dma_start(
+                out=plane[32 * q : 32 * q + 4, :, :].bitcast(I32),
+                in_=scales[:, 4 * q : 4 * q + 4, :].rearrange("z r n -> r z n").bitcast(I32),
+            )
+
+        def load_wa(h, z):
+            rows = wa[512 * z : 512 * (z + 1), cols(h, HALF)]
+            nc.sync.dma_start(out=raw[h, z][:], in_=rows.rearrange("(p j) n -> p j n", j=4))
+
+        def cast(copy, h, z):
+            copy(
+                out=grp[h, z][:].rearrange("p (c i) j -> p c j i", i=4),
+                in_=raw[h, z][:].rearrange("p j (c i) -> p c j i", i=4),
+            )
+
+        def quantize(h, z):
+            nc.vector.quantize_mx(
+                out=wa_w[h, z][:].bitcast(FP8X4),
+                scales=wa_s[h, z][:],
+                in_=grp[h, z][:].rearrange("p n j -> p (n j)"),
+            )
+
+        nc.vector.memset(xt_s[:].bitcast(I32), 0)
+        nc.vector.memset(ws_s[:].bitcast(I32), 0)
+        nc.vector.memset(wc_s[:].bitcast(I32), 0)
+        nc.vector.memset(xs_s[:].bitcast(I32), 0)
+        nc.vector.memset(warm_in[:], 0.0)
+        nc.scalar.activation(out=warm_out[:], in_=warm_in[:], func=ACT.Tanh)
+        make_identity(nc, ident[:])
+
+        load_wa(0, 0)
+        for q in range(4):
+            load_scales(nc.sync, xt_s, xt_scales, q)
+        with nc.allow_non_contiguous_dma(reason="one offset to a partition"):
+            nc.sync.dma_start(out=bias_col[:], in_=bi.rearrange("o (c p) -> p (o c)", p=P))
+        nc.sync.dma_start(out=xt_w[:], in_=xt_words.rearrange("z p n r -> p z (n r)").bitcast(I32))
+        nc.sync.dma_start(out=wc_w[:].bitcast(I32), in_=wc_words.rearrange("z p n -> p z n").bitcast(I32))
+        for q in range(4):
+            load_scales(nc.gpsimd, ws_s, ws_scales, q)
+        for q in range(4):
+            load_scales(nc.sync, wc_s, wc_scales, q)
+        load_wa(0, 1)
+        load_scales(nc.sync, xs_s, xs_scales, 0)
+        nc.sync.dma_start(out=ws_w[:], in_=ws_words[0].rearrange("p n r -> p (n r)").bitcast(I32))
+        nc.sync.dma_start(out=xs_w[:].bitcast(I32), in_=xs_words[0].bitcast(I32))
+        for q in range(1, 4):
+            load_scales(nc.sync, xs_s, xs_scales, q)
+        load_wa(1, 0)
+        load_wa(1, 1)
+
+        bias_ps = ps.tile([P, N], F32, name="bias_ps", tag="T3")
+        for j in range(4):
+            nc.tensor.transpose(bias_ps[:, cols(j)], bias_col[:, j : j + 1].to_broadcast([P, P]), ident[:])
+        cast(nc.scalar.copy, 0, 0)
+        nc.scalar.copy(out=bias_row[:], in_=bias_ps[:])
+        quantize(0, 0)
+
+        at_ps = [ps.tile([P, T], F32, name="at_ps%d" % j, tag="T%d" % j) for j in range(4)]
+
+        def pass_wa(j, z, start, stop):
+            h, c = divmod(j, 2)
+            nc.tensor.matmul_mx(
+                out=at_ps[j][:],
+                lhsT=wa_w[h, z][:, cols(c)].bitcast(FP8X4),
+                lhsT_scale=wa_s[h, z][:, cols(c)],
+                rhs=xt_w[:, z, :].bitcast(FP8X4),
+                rhs_scale=xt_s[:, z, :],
+                start=start,
+                stop=stop,
+            )
+
+        def pass_ws(j, start):
+            nc.tensor.matmul_mx(
+                out=at_ps[j][:],
+                lhsT=ws_w[:, cols(j)].bitcast(FP8X4),
+                lhsT_scale=ws_s[:, 0, cols(j)],
+                rhs=xs_w[:].bitcast(FP4X4),
+                rhs_scale=xs_s[:, 0, :],
+                start=start,
+                stop=False,
+            )
+
+        for j in range(2):
+            pass_wa(j, 0, True, False)
+
+        b_ps = [ps.tile([P, N], F32, name="b_ps%d" % t, tag="A%d" % t) for t in range(4)]
+        for t in range(4):
+            for z in range(2):
+                nc.tensor.matmul_mx(
+                    out=b_ps[t][:],
+                    lhsT=xt_w[:, z, cols(t)].bitcast(FP8X4),
+                    lhsT_scale=xt_s[:, z, cols(t)],
+                    rhs=wc_w[:, z, :].bitcast(FP4X4),
+                    rhs_scale=wc_s[:, z, :],
+                    start=(z == 0),
+                    stop=(z == 1),
+                )
+
+        def add_bias_b(t):
+            nc.vector.tensor_tensor(out=b_sb[t][:], in0=b_ps[t][:], in1=bias_row[:], op=ALU.add)
+
+        cast(nc.scalar.copy, 0, 1)
+        for t in range(3):
+            add_bias_b(t)
+        quantize(0, 1)
+        add_bias_b(3)
+
+        for j in range(2):
+            pass_ws(j, False)
+        for j in range(2):
+            pass_wa(j, 1, False, True)
+        for j in range(2, 4):
+            pass_ws(j, True)
+
+        def add_bias_a_scalar(j):
+            nc.scalar.activation(
+                out=at_sb[j][:], in_=at_ps[j][:], func=ACT.Identity, bias=bias_col[:, j : j + 1]
+            )
+
+        for j in range(2):
+            add_bias_a_scalar(j)
+        cast(nc.vector.tensor_copy, 1, 0)
+        quantize(1, 0)
+        cast(nc.vector.tensor_copy, 1, 1)
+        quantize(1, 1)
+        for j in range(2, 4):
+            pass_wa(j, 0, False, False)
+
+        a_ps = {}
+        for h in range(2):
+            for tp in range(2):
+                a_ps[h, tp] = ps.tile([P, 2, HALF], F32, name="a_ps%d%d" % (h, tp), tag="A%d" % (2 * h + tp))
+
+        def turn(j):
+            h, c = divmod(j, 2)
+            for t in range(4):
+                nc.tensor.transpose(a_ps[h, t // 2][:, t % 2, cols(c)], at_sb[j][:, cols(t)], ident[:])
+
+        def agree(h, t):
+            nc.vector.scalar_tensor_tensor(
+                out=prod[t % 2][:],
+                in0=a_ps[h, t // 2][:, t % 2, :],
+                scalar=2.0 / N,
+                in1=b_sb[t][:, cols(h, HALF)],
+                op0=ALU.mult,
+                op1=ALU.mult,
+                accum_out=part[h][:, t : t + 1],
+            )
+
+        turn(0)
+        turn(1)
+        for j in range(2, 4):
+            pass_wa(j, 1, False, True)
+        add_bias_a_scalar(2)
+        agree(0, 0)
+        agree(0, 1)
+        nc.vector.tensor_scalar(
+            out=at_sb[3][:], in0=at_ps[3][:], scalar1=bias_col[:, 3:4], scalar2=None, op0=ALU.add
+        )
+        agree(0, 2)
+        agree(0, 3)
+        turn(2)
+        turn(3)
+        for t in range(4):
+            agree(1, t)
+            nc.scalar.activation(
+                out=gate[:, t : t + 1], in_=part[1][:, t : t + 1], func=ACT.Tanh, bias=part[0][:, t : t + 1]
+            )
+        for t in range(4):
+            for h in range(2):
+                nc.vector.scalar_tensor_tensor(
+                    out=y_sb[t][:, cols(h, HALF)],
+                    in0=b_sb[t][:, cols(h, HALF)],
+                    scalar=gate[:, t : t + 1],
+                    in1=a_ps[h, t // 2][:, t % 2, :],
+                    op0=ALU.mult,
+                    op1=ALU.add,
+                )
+            nc.sync.dma_start(out=out[cols(t), :], in_=y_sb[t][:])

@@ -17,6 +17,7 @@ ACT = mybir.ActivationFunctionType
 
 P = 128
 HALF = 256
+SCALAR_COLS = 144
 
 
 def tile_mix_rows_heard_by_agreement_kernel(
@@ -50,7 +51,7 @@ def tile_mix_rows_heard_by_agreement_kernel(
         wa_w = {k: tile("wa_w%d%d" % k, [P, HALF], I32) for k in keys}
         wa_s = {k: tile("wa_s%d%d" % k, [P, HALF], U8) for k in keys}
         b_sb = [tile("b_sb%d" % t, [P, N], F32) for t in range(4)]
-        at_sb = [tile("at_sb%d" % j, [P, T], F32) for j in range(4)]
+        a_sb = tile("a_sb", [P, 4, N], F32)
         y_sb = [tile("y_sb%d" % t, [P, N], F32) for t in range(4)]
         prod = [tile("prod%d" % i, [P, HALF], F32) for i in range(2)]
         part = [tile("part%d" % h, [P, 4], F32) for h in range(2)]
@@ -59,20 +60,28 @@ def tile_mix_rows_heard_by_agreement_kernel(
         def cols(i, width=P):
             return slice(i * width, (i + 1) * width)
 
-        def load_scales(engine, plane, scales, q):
+        def load_scales(engine, plane, scales, r):
             engine.dma_start(
-                out=plane[32 * q : 32 * q + 4, :, :].bitcast(I32),
-                in_=scales[:, 4 * q : 4 * q + 4, :].rearrange("z r n -> r z n").bitcast(I32),
+                out=plane[r:P:32, :, :].bitcast(I32),
+                in_=scales[:, r:16:4, :].rearrange("z q n -> q z n").bitcast(I32),
             )
 
         def load_wa(h, z):
             rows = wa[512 * z : 512 * (z + 1), cols(h, HALF)]
             nc.sync.dma_start(out=raw[h, z][:], in_=rows.rearrange("(p j) n -> p j n", j=4))
 
-        def cast(copy, h, z):
-            copy(
-                out=grp[h, z][:].rearrange("p (c i) j -> p c j i", i=4),
-                in_=raw[h, z][:].rearrange("p j (c i) -> p c j i", i=4),
+        def cast(h, z):
+            nc.scalar.copy(
+                out=grp[h, z][:, :SCALAR_COLS, :].rearrange("p (c i) j -> p c j i", i=4),
+                in_=raw[h, z][:, :, :SCALAR_COLS].rearrange("p j (c i) -> p c j i", i=4),
+            )
+            nc.gpsimd.tensor_scalar(
+                out=grp[h, z][:, SCALAR_COLS:, :],
+                in0=raw[h, z][:, :, SCALAR_COLS:].rearrange("p j c -> p c j"),
+                scalar1=1.0,
+                scalar2=0.0,
+                op0=ALU.mult,
+                op1=ALU.add,
             )
 
         def quantize(h, z):
@@ -83,70 +92,41 @@ def tile_mix_rows_heard_by_agreement_kernel(
             )
 
         nc.vector.memset(xt_s[:].bitcast(I32), 0)
-        nc.vector.memset(ws_s[:].bitcast(I32), 0)
         nc.vector.memset(wc_s[:].bitcast(I32), 0)
+        nc.vector.memset(ws_s[:].bitcast(I32), 0)
         nc.vector.memset(xs_s[:].bitcast(I32), 0)
         nc.vector.memset(warm_in[:], 0.0)
         nc.scalar.activation(out=warm_out[:], in_=warm_in[:], func=ACT.Tanh)
         make_identity(nc, ident[:])
 
-        load_wa(0, 0)
-        for q in range(4):
-            load_scales(nc.sync, xt_s, xt_scales, q)
         with nc.allow_non_contiguous_dma(reason="one offset to a partition"):
             nc.sync.dma_start(out=bias_col[:], in_=bi.rearrange("o (c p) -> p (o c)", p=P))
+        for r in range(4):
+            load_scales(nc.sync, xt_s, xt_scales, r)
         nc.sync.dma_start(out=xt_w[:], in_=xt_words.rearrange("z p n r -> p z (n r)").bitcast(I32))
         nc.sync.dma_start(out=wc_w[:].bitcast(I32), in_=wc_words.rearrange("z p n -> p z n").bitcast(I32))
-        for q in range(4):
-            load_scales(nc.gpsimd, ws_s, ws_scales, q)
-        for q in range(4):
-            load_scales(nc.sync, wc_s, wc_scales, q)
+        for r in range(4):
+            load_scales(nc.gpsimd, ws_s, ws_scales, r)
+        for r in range(4):
+            load_scales(nc.sync, wc_s, wc_scales, r)
+        load_wa(0, 0)
         load_wa(0, 1)
-        load_scales(nc.sync, xs_s, xs_scales, 0)
+        for r in range(4):
+            load_scales(nc.sync, xs_s, xs_scales, r)
         nc.sync.dma_start(out=ws_w[:], in_=ws_words[0].rearrange("p n r -> p (n r)").bitcast(I32))
         nc.sync.dma_start(out=xs_w[:].bitcast(I32), in_=xs_words[0].bitcast(I32))
-        for q in range(1, 4):
-            load_scales(nc.sync, xs_s, xs_scales, q)
         load_wa(1, 0)
         load_wa(1, 1)
 
-        bias_ps = ps.tile([P, N], F32, name="bias_ps", tag="T3")
+        bias_ps = ps.tile([P, N], F32, name="bias_ps", tag="A11")
         for j in range(4):
             nc.tensor.transpose(bias_ps[:, cols(j)], bias_col[:, j : j + 1].to_broadcast([P, P]), ident[:])
-        cast(nc.scalar.copy, 0, 0)
         nc.scalar.copy(out=bias_row[:], in_=bias_ps[:])
-        quantize(0, 0)
 
-        at_ps = [ps.tile([P, T], F32, name="at_ps%d" % j, tag="T%d" % j) for j in range(4)]
+        b_ps = [ps.tile([P, N], F32, name="b_ps%d" % t, tag="B%d" % t) for t in range(4)]
+        a_ps = {k: ps.tile([P, 2, HALF], F32, name="a_ps%d%d" % k, tag="A%d%d" % k) for k in keys}
 
-        def pass_wa(j, z, start, stop):
-            h, c = divmod(j, 2)
-            nc.tensor.matmul_mx(
-                out=at_ps[j][:],
-                lhsT=wa_w[h, z][:, cols(c)].bitcast(FP8X4),
-                lhsT_scale=wa_s[h, z][:, cols(c)],
-                rhs=xt_w[:, z, :].bitcast(FP8X4),
-                rhs_scale=xt_s[:, z, :],
-                start=start,
-                stop=stop,
-            )
-
-        def pass_ws(j, start):
-            nc.tensor.matmul_mx(
-                out=at_ps[j][:],
-                lhsT=ws_w[:, cols(j)].bitcast(FP8X4),
-                lhsT_scale=ws_s[:, 0, cols(j)],
-                rhs=xs_w[:].bitcast(FP4X4),
-                rhs_scale=xs_s[:, 0, :],
-                start=start,
-                stop=False,
-            )
-
-        for j in range(2):
-            pass_wa(j, 0, True, False)
-
-        b_ps = [ps.tile([P, N], F32, name="b_ps%d" % t, tag="A%d" % t) for t in range(4)]
-        for t in range(4):
+        def product_b(t):
             for z in range(2):
                 nc.tensor.matmul_mx(
                     out=b_ps[t][:],
@@ -158,50 +138,46 @@ def tile_mix_rows_heard_by_agreement_kernel(
                     stop=(z == 1),
                 )
 
-        def add_bias_b(t):
+        def product_wa(h, z, first=False, last=False):
+            for t in range(4):
+                nc.tensor.matmul_mx(
+                    out=a_ps[h, t // 2][:, t % 2, :],
+                    lhsT=xt_w[:, z, cols(t)].bitcast(FP8X4),
+                    lhsT_scale=xt_s[:, z, cols(t)],
+                    rhs=wa_w[h, z][:].bitcast(FP8X4),
+                    rhs_scale=wa_s[h, z][:],
+                    start=first and t % 2 == 0,
+                    stop=last and t % 2 == 1,
+                )
+
+        def product_ws(h, first=False, last=False):
+            for t in range(4):
+                for c in range(2):
+                    nc.tensor.matmul_mx(
+                        out=a_ps[h, t // 2][:, t % 2, cols(c)],
+                        lhsT=xs_w[:, cols(t, 2 * P)].bitcast(FP4X4),
+                        lhsT_scale=xs_s[:, 0, cols(t)],
+                        rhs=ws_w[:, cols(2 * h + c)].bitcast(FP8X4),
+                        rhs_scale=ws_s[:, 0, cols(2 * h + c)],
+                        start=first and t % 2 == 0 and c == 0,
+                        stop=last and t % 2 == 1 and c == 1,
+                    )
+
+        def offset_b(t):
             nc.vector.tensor_tensor(out=b_sb[t][:], in0=b_ps[t][:], in1=bias_row[:], op=ALU.add)
 
-        cast(nc.scalar.copy, 0, 1)
-        for t in range(3):
-            add_bias_b(t)
-        quantize(0, 1)
-        add_bias_b(3)
-
-        for j in range(2):
-            pass_ws(j, False)
-        for j in range(2):
-            pass_wa(j, 1, False, True)
-        for j in range(2, 4):
-            pass_ws(j, True)
-
-        def add_bias_a_scalar(j):
-            nc.scalar.activation(
-                out=at_sb[j][:], in_=at_ps[j][:], func=ACT.Identity, bias=bias_col[:, j : j + 1]
+        def offset_a(h, tp):
+            nc.vector.tensor_tensor(
+                out=a_sb[:, cols(tp, 2), cols(h, HALF)],
+                in0=a_ps[h, tp][:],
+                in1=bias_row[:, cols(h, HALF)].unsqueeze(1).to_broadcast([P, 2, HALF]),
+                op=ALU.add,
             )
-
-        for j in range(2):
-            add_bias_a_scalar(j)
-        cast(nc.vector.tensor_copy, 1, 0)
-        quantize(1, 0)
-        cast(nc.vector.tensor_copy, 1, 1)
-        quantize(1, 1)
-        for j in range(2, 4):
-            pass_wa(j, 0, False, False)
-
-        a_ps = {}
-        for h in range(2):
-            for tp in range(2):
-                a_ps[h, tp] = ps.tile([P, 2, HALF], F32, name="a_ps%d%d" % (h, tp), tag="A%d" % (2 * h + tp))
-
-        def turn(j):
-            h, c = divmod(j, 2)
-            for t in range(4):
-                nc.tensor.transpose(a_ps[h, t // 2][:, t % 2, cols(c)], at_sb[j][:, cols(t)], ident[:])
 
         def agree(h, t):
             nc.vector.scalar_tensor_tensor(
                 out=prod[t % 2][:],
-                in0=a_ps[h, t // 2][:, t % 2, :],
+                in0=a_sb[:, t, cols(h, HALF)],
                 scalar=2.0 / N,
                 in1=b_sb[t][:, cols(h, HALF)],
                 op0=ALU.mult,
@@ -209,33 +185,57 @@ def tile_mix_rows_heard_by_agreement_kernel(
                 accum_out=part[h][:, t : t + 1],
             )
 
-        turn(0)
-        turn(1)
-        for j in range(2, 4):
-            pass_wa(j, 1, False, True)
-        add_bias_a_scalar(2)
-        agree(0, 0)
-        agree(0, 1)
-        nc.vector.tensor_scalar(
-            out=at_sb[3][:], in0=at_ps[3][:], scalar1=bias_col[:, 3:4], scalar2=None, op0=ALU.add
-        )
-        agree(0, 2)
-        agree(0, 3)
-        turn(2)
-        turn(3)
-        for t in range(4):
+        def finish_gate(t):
             agree(1, t)
             nc.scalar.activation(
                 out=gate[:, t : t + 1], in_=part[1][:, t : t + 1], func=ACT.Tanh, bias=part[0][:, t : t + 1]
             )
-        for t in range(4):
-            for h in range(2):
+
+        def blend(t, pieces):
+            width = N // pieces
+            for i in range(pieces):
                 nc.vector.scalar_tensor_tensor(
-                    out=y_sb[t][:, cols(h, HALF)],
-                    in0=b_sb[t][:, cols(h, HALF)],
+                    out=y_sb[t][:, cols(i, width)],
+                    in0=b_sb[t][:, cols(i, width)],
                     scalar=gate[:, t : t + 1],
-                    in1=a_ps[h, t // 2][:, t % 2, :],
+                    in1=a_sb[:, t, cols(i, width)],
                     op0=ALU.mult,
                     op1=ALU.add,
                 )
-            nc.sync.dma_start(out=out[cols(t), :], in_=y_sb[t][:])
+                nc.sync.dma_start(out=out[cols(t), cols(i, width)], in_=y_sb[t][:, cols(i, width)])
+
+        for t in range(3):
+            product_b(t)
+        cast(0, 0)
+        offset_b(0)
+        quantize(0, 0)
+        cast(0, 1)
+        offset_b(1)
+        quantize(0, 1)
+        offset_b(2)
+        product_wa(0, 0, first=True)
+        product_b(3)
+        offset_b(3)
+        product_wa(0, 1)
+        product_ws(0, last=True)
+        product_ws(1, first=True)
+        cast(1, 0)
+        offset_a(0, 0)
+        quantize(1, 0)
+        cast(1, 1)
+        offset_a(0, 1)
+        product_wa(1, 0)
+        quantize(1, 1)
+        product_wa(1, 1, last=True)
+        for t in range(4):
+            agree(0, t)
+        offset_a(1, 0)
+        finish_gate(0)
+        finish_gate(1)
+        offset_a(1, 1)
+        blend(0, 1)
+        finish_gate(2)
+        blend(1, 1)
+        finish_gate(3)
+        blend(2, 2)
+        blend(3, 2)

@@ -17,7 +17,7 @@ ACT = mybir.ActivationFunctionType
 
 P = 128
 HALF = 256
-SCALAR_COLS = 144
+WARM_PASSES = 4
 
 
 def tile_mix_rows_heard_by_agreement_kernel(
@@ -70,18 +70,10 @@ def tile_mix_rows_heard_by_agreement_kernel(
             rows = wa[512 * z : 512 * (z + 1), cols(h, HALF)]
             nc.sync.dma_start(out=raw[h, z][:], in_=rows.rearrange("(p j) n -> p j n", j=4))
 
-        def cast(h, z):
-            nc.scalar.copy(
-                out=grp[h, z][:, :SCALAR_COLS, :].rearrange("p (c i) j -> p c j i", i=4),
-                in_=raw[h, z][:, :, :SCALAR_COLS].rearrange("p j (c i) -> p c j i", i=4),
-            )
-            nc.gpsimd.tensor_scalar(
-                out=grp[h, z][:, SCALAR_COLS:, :],
-                in0=raw[h, z][:, :, SCALAR_COLS:].rearrange("p j c -> p c j"),
-                scalar1=1.0,
-                scalar2=0.0,
-                op0=ALU.mult,
-                op1=ALU.add,
+        def cast(copy, h, z):
+            copy(
+                out=grp[h, z][:].rearrange("p (c i) j -> p c j i", i=2),
+                in_=raw[h, z][:].rearrange("p j (c i) -> p c j i", i=2),
             )
 
         def quantize(h, z):
@@ -91,37 +83,51 @@ def tile_mix_rows_heard_by_agreement_kernel(
                 in_=grp[h, z][:].rearrange("p n j -> p (n j)"),
             )
 
-        nc.vector.memset(xt_s[:].bitcast(I32), 0)
-        nc.vector.memset(wc_s[:].bitcast(I32), 0)
-        nc.vector.memset(ws_s[:].bitcast(I32), 0)
-        nc.vector.memset(xs_s[:].bitcast(I32), 0)
+        nc.gpsimd.memset(xt_s[:].bitcast(I32), 0)
         nc.vector.memset(warm_in[:], 0.0)
+        nc.vector.memset(ws_s[:].bitcast(I32), 0)
+        nc.vector.memset(wc_s[:].bitcast(I32), 0)
+        nc.vector.memset(xs_s[:].bitcast(I32), 0)
         nc.scalar.activation(out=warm_out[:], in_=warm_in[:], func=ACT.Tanh)
         make_identity(nc, ident[:])
 
-        with nc.allow_non_contiguous_dma(reason="one offset to a partition"):
-            nc.sync.dma_start(out=bias_col[:], in_=bi.rearrange("o (c p) -> p (o c)", p=P))
+        nc.sync.dma_start(out=bias_col[:], in_=bi.rearrange("o (p c) -> p (o c)", p=P))
+        nc.sync.dma_start(out=xt_w[:], in_=xt_words.rearrange("z p n r -> p z (n r)").bitcast(I32))
         for r in range(4):
             load_scales(nc.sync, xt_s, xt_scales, r)
-        nc.sync.dma_start(out=xt_w[:], in_=xt_words.rearrange("z p n r -> p z (n r)").bitcast(I32))
         nc.sync.dma_start(out=wc_w[:].bitcast(I32), in_=wc_words.rearrange("z p n -> p z n").bitcast(I32))
+        load_wa(0, 0)
         for r in range(4):
             load_scales(nc.gpsimd, ws_s, ws_scales, r)
         for r in range(4):
             load_scales(nc.sync, wc_s, wc_scales, r)
-        load_wa(0, 0)
         load_wa(0, 1)
-        for r in range(4):
-            load_scales(nc.sync, xs_s, xs_scales, r)
+        load_scales(nc.sync, xs_s, xs_scales, 0)
         nc.sync.dma_start(out=ws_w[:], in_=ws_words[0].rearrange("p n r -> p (n r)").bitcast(I32))
         nc.sync.dma_start(out=xs_w[:].bitcast(I32), in_=xs_words[0].bitcast(I32))
+        for r in range(1, 4):
+            load_scales(nc.sync, xs_s, xs_scales, r)
         load_wa(1, 0)
         load_wa(1, 1)
 
         bias_ps = ps.tile([P, N], F32, name="bias_ps", tag="A11")
         for j in range(4):
             nc.tensor.transpose(bias_ps[:, cols(j)], bias_col[:, j : j + 1].to_broadcast([P, P]), ident[:])
-        nc.scalar.copy(out=bias_row[:], in_=bias_ps[:])
+        nc.scalar.copy(
+            out=bias_row[:].rearrange("p (m c) -> p m c", c=4), in_=bias_ps[:].rearrange("p (c m) -> p m c", c=4)
+        )
+
+        warm_ps = ps.tile([P, T], F32, name="warm_ps", tag="A10")
+        for i in range(WARM_PASSES):
+            nc.tensor.matmul_mx(
+                out=warm_ps[:],
+                lhsT=xt_w[:, 0, cols(0)].bitcast(FP8X4),
+                lhsT_scale=xt_s[:, 0, cols(0)],
+                rhs=xt_w[:, 0, :].bitcast(FP8X4),
+                rhs_scale=xt_s[:, 0, :],
+                start=True,
+                stop=True,
+            )
 
         b_ps = [ps.tile([P, N], F32, name="b_ps%d" % t, tag="B%d" % t) for t in range(4)]
         a_ps = {k: ps.tile([P, 2, HALF], F32, name="a_ps%d%d" % k, tag="A%d%d" % k) for k in keys}
@@ -206,28 +212,28 @@ def tile_mix_rows_heard_by_agreement_kernel(
 
         for t in range(3):
             product_b(t)
-        cast(0, 0)
-        offset_b(0)
+        cast(nc.vector.tensor_copy, 0, 0)
         quantize(0, 0)
-        cast(0, 1)
-        offset_b(1)
+        cast(nc.scalar.copy, 0, 1)
+        for t in range(3):
+            offset_b(t)
         quantize(0, 1)
-        offset_b(2)
         product_wa(0, 0, first=True)
         product_b(3)
         offset_b(3)
-        product_wa(0, 1)
-        product_ws(0, last=True)
+        product_ws(0)
+        product_wa(0, 1, last=True)
         product_ws(1, first=True)
-        cast(1, 0)
+        cast(nc.scalar.copy, 1, 0)
         offset_a(0, 0)
         quantize(1, 0)
-        cast(1, 1)
+        cast(nc.scalar.copy, 1, 1)
         offset_a(0, 1)
         product_wa(1, 0)
+        agree(0, 0)
         quantize(1, 1)
         product_wa(1, 1, last=True)
-        for t in range(4):
+        for t in range(1, 4):
             agree(0, t)
         offset_a(1, 0)
         finish_gate(0)

@@ -56,6 +56,8 @@ def tile_mix_rows_heard_by_agreement_kernel(
         prod = [tile("prod%d" % i, [P, HALF], F32) for i in range(2)]
         part = [tile("part%d" % h, [P, 4], F32) for h in range(2)]
         gate = tile("gate", [P, 4], F32)
+        bias_n = tile("bias_n", [P, 2], F32)
+        at_sb = [tile("at_sb%d" % j, [P, HALF], F32) for j in range(2)]
 
         def cols(i, width=P):
             return slice(i * width, (i + 1) * width)
@@ -130,7 +132,7 @@ def tile_mix_rows_heard_by_agreement_kernel(
             )
 
         b_ps = [ps.tile([P, N], F32, name="b_ps%d" % t, tag="B%d" % t) for t in range(4)]
-        a_ps = {k: ps.tile([P, 2, HALF], F32, name="a_ps%d%d" % k, tag="A%d%d" % k) for k in keys}
+        a_ps = {k: ps.tile([P, 2, HALF], F32, name="a_ps%d%d" % k, tag="A%d%d" % k) for k in keys[:3]}
 
         def product_b(t):
             for z in range(2):
@@ -145,7 +147,7 @@ def tile_mix_rows_heard_by_agreement_kernel(
                 )
 
         def product_wa(h, z, first=False, last=False):
-            for t in range(4):
+            for t in range(4 - 2 * h):
                 nc.tensor.matmul_mx(
                     out=a_ps[h, t // 2][:, t % 2, :],
                     lhsT=xt_w[:, z, cols(t)].bitcast(FP8X4),
@@ -157,7 +159,7 @@ def tile_mix_rows_heard_by_agreement_kernel(
                 )
 
         def product_ws(h, first=False, last=False):
-            for t in range(4):
+            for t in range(4 - 2 * h):
                 for c in range(2):
                     nc.tensor.matmul_mx(
                         out=a_ps[h, t // 2][:, t % 2, cols(c)],
@@ -168,6 +170,37 @@ def tile_mix_rows_heard_by_agreement_kernel(
                         start=first and t % 2 == 0 and c == 0,
                         stop=last and t % 2 == 1 and c == 1,
                     )
+
+        def a_view(h, t):
+            if h == 1 and t >= 2:
+                return turned["a"][:, t - 2, :]
+            return a_sb[:, t, cols(h, HALF)]
+
+        def turned_ws(j):
+            for t in range(2, 4):
+                nc.tensor.matmul_mx(
+                    out=at_ps[j][:, cols(t - 2)],
+                    lhsT=ws_w[:, cols(2 + j)].bitcast(FP8X4),
+                    lhsT_scale=ws_s[:, 0, cols(2 + j)],
+                    rhs=xs_w[:, cols(t, 2 * P)].bitcast(FP4X4),
+                    rhs_scale=xs_s[:, 0, cols(t)],
+                    start=(t == 2),
+                    stop=False,
+                )
+
+        def turned_wa(j, z):
+            nc.tensor.matmul_mx(
+                out=at_ps[j][:],
+                lhsT=wa_w[1, z][:, cols(j)].bitcast(FP8X4),
+                lhsT_scale=wa_s[1, z][:, cols(j)],
+                rhs=xt_w[:, z, cols(1, HALF)].bitcast(FP8X4),
+                rhs_scale=xt_s[:, z, cols(1, HALF)],
+                start=False,
+                stop=(z == 1),
+            )
+
+        turned = {}
+        at_ps = {}
 
         def offset_b(t):
             nc.vector.tensor_tensor(out=b_sb[t][:], in0=b_ps[t][:], in1=bias_row[:], op=ALU.add)
@@ -183,7 +216,7 @@ def tile_mix_rows_heard_by_agreement_kernel(
         def agree(h, t):
             nc.vector.scalar_tensor_tensor(
                 out=prod[t % 2][:],
-                in0=a_sb[:, t, cols(h, HALF)],
+                in0=a_view(h, t),
                 scalar=2.0 / N,
                 in1=b_sb[t][:, cols(h, HALF)],
                 op0=ALU.mult,
@@ -204,7 +237,7 @@ def tile_mix_rows_heard_by_agreement_kernel(
                     out=y_sb[t][:, cols(i, width)],
                     in0=b_sb[t][:, cols(i, width)],
                     scalar=gate[:, t : t + 1],
-                    in1=a_sb[:, t, cols(i, width)],
+                    in1=a_sb[:, t, :] if pieces == 1 else a_view(i, t),
                     op0=ALU.mult,
                     op1=ALU.add,
                 )
@@ -224,21 +257,37 @@ def tile_mix_rows_heard_by_agreement_kernel(
         product_ws(0)
         product_wa(0, 1, last=True)
         product_ws(1, first=True)
+        for j, tag in enumerate(("A11", "B2")):
+            at_ps[j] = ps.tile([P, HALF], F32, name="at_ps%d" % j, tag=tag)
+            turned_ws(j)
+        bias_n_ps = ps.tile([P, 2, P], F32, name="bias_n_ps", tag="B1")
+        for j in range(2):
+            nc.tensor.transpose(bias_n_ps[:, j, :], bias_row[:, cols(2 + j)], ident[:])
         cast(nc.scalar.copy, 1, 0)
         offset_a(0, 0)
         quantize(1, 0)
         cast(nc.scalar.copy, 1, 1)
+        nc.scalar.copy(out=bias_n[:], in_=bias_n_ps[:, :, 0])
         offset_a(0, 1)
         product_wa(1, 0)
+        for j in range(2):
+            turned_wa(j, 0)
         agree(0, 0)
         quantize(1, 1)
         product_wa(1, 1, last=True)
-        for t in range(1, 4):
-            agree(0, t)
+        for j in range(2):
+            turned_wa(j, 1)
+        turned["a"] = ps.tile([P, 2, HALF], F32, name="a_turned", tag="B0")
+        for j in range(2):
+            nc.scalar.activation(out=at_sb[j][:], in_=at_ps[j][:], func=ACT.Identity, bias=bias_n[:, j : j + 1])
+            for t in range(2):
+                nc.tensor.transpose(turned["a"][:, t, cols(j)], at_sb[j][:, cols(t)], ident[:])
+        agree(0, 1)
+        agree(0, 2)
         offset_a(1, 0)
+        agree(0, 3)
         finish_gate(0)
         finish_gate(1)
-        offset_a(1, 1)
         blend(0, 1)
         finish_gate(2)
         blend(1, 1)

from contextlib import ExitStack

import concourse.mybir as mybir
from concourse.masks import make_identity

K, L, T, N = 1024, 512, 512, 512
FLOPS = 2 * T * N * (2 * K + L)

F32 = mybir.dt.float32
BF16 = mybir.dt.bfloat16
I32 = mybir.dt.int32
U8 = mybir.dt.uint8
FP8X4 = mybir.dt.float8_e4m3fn_x4
FP4X4 = mybir.dt.float4_e2m1fn_x4
ALU = mybir.AluOpType
ACT = mybir.ActivationFunctionType

P = 128
HALF = 256
WARM_PASSES = 4


def tile_mix_rows_heard_by_agreement_kernel(
    tc, xt_words, xt_scales, wa, xs_words, xs_scales, ws_words, ws_scales, wc_words, wc_scales, bi, out
):
    nc = tc.nc
    with ExitStack() as ctx:
        sb = ctx.enter_context(tc.tile_pool(name="sb", bufs=1))
        ps = ctx.enter_context(tc.psum_pool(name="ps", bufs=1))
        ctx.enter_context(tc.manual_schedule())

        def tile(name, shape, dtype):
            return sb.tile(shape, dtype, name=name, tag=name, align_bytes=64)

        xt_w = tile("xt_w", [P, 2, T], I32)
        xt_s = tile("xt_s", [P, 2, T], U8)
        wc_w = tile("wc_w", [P, 2, 2 * N], U8)
        wc_s = tile("wc_s", [P, 2, N], U8)
        xs_w = tile("xs_w", [P, 2 * T], U8)
        xs_s = tile("xs_s", [P, 1, T], U8)
        ws_w = tile("ws_w", [P, N], I32)
        ws_s = tile("ws_s", [P, 1, N], U8)
        bias_col = tile("bias_col", [P, 4], F32)
        bias_row = tile("bias_row", [P, N], F32)
        ident = tile("ident", [P, P], F32)
        warm_in = tile("warm_in", [P, 1], F32)
        warm_out = tile("warm_out", [P, 1], F32)
        keys = [(h, z) for h in range(2) for z in range(2)]
        raw = {k: tile("raw%d%d" % k, [P, 4, HALF], F32) for k in keys}
        grp = {k: tile("grp%d%d" % k, [P, HALF, 4], BF16) for k in keys}
        wa_w = {k: tile("wa_w%d%d" % k, [P, HALF], I32) for k in keys}
        wa_s = {k: tile("wa_s%d%d" % k, [P, HALF], U8) for k in keys}
        b_sb = [tile("b_sb%d" % t, [P, N], F32) for t in range(4)]
        a_sb = tile("a_sb", [P, 4, N], F32)
        y_sb = [tile("y_sb%d" % t, [P, N], F32) for t in range(4)]
        prod = [tile("prod%d" % i, [P, HALF], F32) for i in range(2)]
        part = [tile("part%d" % h, [P, 4], F32) for h in range(2)]
        gate = tile("gate", [P, 4], F32)
        bias_n = tile("bias_n", [P, 2], F32)
        at_sb = [tile("at_sb%d" % j, [P, HALF], F32) for j in range(2)]

        def cols(i, width=P):
            return slice(i * width, (i + 1) * width)

        def load_scales(engine, plane, scales, r):
            engine.dma_start(
                out=plane[r:P:32, :, :].bitcast(I32),
                in_=scales[:, r:16:4, :].rearrange("z q n -> q z n").bitcast(I32),
            )

        def load_wa(h, z):
            rows = wa[512 * z : 512 * (z + 1), cols(h, HALF)]
            nc.sync.dma_start(out=raw[h, z][:], in_=rows.rearrange("(p j) n -> p j n", j=4))

        def cast(copy, h, z):
            copy(
                out=grp[h, z][:].rearrange("p (c i) j -> p c j i", i=2),
                in_=raw[h, z][:].rearrange("p j (c i) -> p c j i", i=2),
            )

        def quantize(h, z):
            nc.vector.quantize_mx(
                out=wa_w[h, z][:].bitcast(FP8X4),
                scales=wa_s[h, z][:],
                in_=grp[h, z][:].rearrange("p n j -> p (n j)"),
            )

        nc.gpsimd.memset(xt_s[:].bitcast(I32), 0)
        nc.vector.memset(warm_in[:], 0.0)
        nc.vector.memset(ws_s[:].bitcast(I32), 0)
        nc.vector.memset(wc_s[:].bitcast(I32), 0)
        nc.vector.memset(xs_s[:].bitcast(I32), 0)
        nc.scalar.activation(out=warm_out[:], in_=warm_in[:], func=ACT.Tanh)
        make_identity(nc, ident[:])

        nc.sync.dma_start(out=bias_col[:], in_=bi.rearrange("o (p c) -> p (o c)", p=P))
        nc.sync.dma_start(out=xt_w[:], in_=xt_words.rearrange("z p n r -> p z (n r)").bitcast(I32))
        for r in range(4):
            load_scales(nc.sync, xt_s, xt_scales, r)
        nc.sync.dma_start(out=wc_w[:].bitcast(I32), in_=wc_words.rearrange("z p n -> p z n").bitcast(I32))
        load_wa(0, 0)
        for r in range(4):
            load_scales(nc.gpsimd, ws_s, ws_scales, r)
        for r in range(4):
            load_scales(nc.sync, wc_s, wc_scales, r)
        load_wa(0, 1)
        load_scales(nc.sync, xs_s, xs_scales, 0)
        nc.sync.dma_start(out=ws_w[:], in_=ws_words[0].rearrange("p n r -> p (n r)").bitcast(I32))
        nc.sync.dma_start(out=xs_w[:].bitcast(I32), in_=xs_words[0].bitcast(I32))
        for r in range(1, 4):
            load_scales(nc.sync, xs_s, xs_scales, r)
        load_wa(1, 0)
        load_wa(1, 1)

        bias_ps = ps.tile([P, N], F32, name="bias_ps", tag="A11")
        for j in range(4):
            nc.tensor.transpose(bias_ps[:, cols(j)], bias_col[:, j : j + 1].to_broadcast([P, P]), ident[:])
        nc.scalar.copy(
            out=bias_row[:].rearrange("p (m c) -> p m c", c=4), in_=bias_ps[:].rearrange("p (c m) -> p m c", c=4)
        )

        warm_ps = ps.tile([P, T], F32, name="warm_ps", tag="A10")
        for i in range(WARM_PASSES):
            nc.tensor.matmul_mx(
                out=warm_ps[:],
                lhsT=xt_w[:, 0, cols(0)].bitcast(FP8X4),
                lhsT_scale=xt_s[:, 0, cols(0)],
                rhs=xt_w[:, 0, :].bitcast(FP8X4),
                rhs_scale=xt_s[:, 0, :],
                start=True,
                stop=True,
            )

        b_ps = [ps.tile([P, N], F32, name="b_ps%d" % t, tag="B%d" % t) for t in range(4)]
        a_ps = {k: ps.tile([P, 2, HALF], F32, name="a_ps%d%d" % k, tag="A%d%d" % k) for k in keys[:3]}

        def product_b(t):
            for z in range(2):
                nc.tensor.matmul_mx(
                    out=b_ps[t][:],
                    lhsT=xt_w[:, z, cols(t)].bitcast(FP8X4),
                    lhsT_scale=xt_s[:, z, cols(t)],
                    rhs=wc_w[:, z, :].bitcast(FP4X4),
                    rhs_scale=wc_s[:, z, :],
                    start=(z == 0),
                    stop=(z == 1),
                )

        def product_wa(h, z, first=False, last=False):
            for t in range(4 - 2 * h):
                nc.tensor.matmul_mx(
                    out=a_ps[h, t // 2][:, t % 2, :],
                    lhsT=xt_w[:, z, cols(t)].bitcast(FP8X4),
                    lhsT_scale=xt_s[:, z, cols(t)],
                    rhs=wa_w[h, z][:].bitcast(FP8X4),
                    rhs_scale=wa_s[h, z][:],
                    start=first and t % 2 == 0,
                    stop=last and t % 2 == 1,
                )

        def product_ws(h, first=False, last=False):
            for t in range(4 - 2 * h):
                for c in range(2):
                    nc.tensor.matmul_mx(
                        out=a_ps[h, t // 2][:, t % 2, cols(c)],
                        lhsT=xs_w[:, cols(t, 2 * P)].bitcast(FP4X4),
                        lhsT_scale=xs_s[:, 0, cols(t)],
                        rhs=ws_w[:, cols(2 * h + c)].bitcast(FP8X4),
                        rhs_scale=ws_s[:, 0, cols(2 * h + c)],
                        start=first and t % 2 == 0 and c == 0,
                        stop=last and t % 2 == 1 and c == 1,
                    )

        def a_view(h, t):
            if h == 1 and t >= 2:
                return turned["a"][:, t - 2, :]
            return a_sb[:, t, cols(h, HALF)]

        def turned_ws(j):
            for t in range(2, 4):
                nc.tensor.matmul_mx(
                    out=at_ps[j][:, cols(t - 2)],
                    lhsT=ws_w[:, cols(2 + j)].bitcast(FP8X4),
                    lhsT_scale=ws_s[:, 0, cols(2 + j)],
                    rhs=xs_w[:, cols(t, 2 * P)].bitcast(FP4X4),
                    rhs_scale=xs_s[:, 0, cols(t)],
                    start=(t == 2),
                    stop=False,
                )

        def turned_wa(j, z):
            nc.tensor.matmul_mx(
                out=at_ps[j][:],
                lhsT=wa_w[1, z][:, cols(j)].bitcast(FP8X4),
                lhsT_scale=wa_s[1, z][:, cols(j)],
                rhs=xt_w[:, z, cols(1, HALF)].bitcast(FP8X4),
                rhs_scale=xt_s[:, z, cols(1, HALF)],
                start=False,
                stop=(z == 1),
            )

        turned = {}
        at_ps = {}

        def offset_b(t):
            nc.vector.tensor_tensor(out=b_sb[t][:], in0=b_ps[t][:], in1=bias_row[:], op=ALU.add)

        def offset_a(h, tp):
            nc.vector.tensor_tensor(
                out=a_sb[:, cols(tp, 2), cols(h, HALF)],
                in0=a_ps[h, tp][:],
                in1=bias_row[:, cols(h, HALF)].unsqueeze(1).to_broadcast([P, 2, HALF]),
                op=ALU.add,
            )

        def agree(h, t):
            nc.vector.scalar_tensor_tensor(
                out=prod[t % 2][:],
                in0=a_view(h, t),
                scalar=2.0 / N,
                in1=b_sb[t][:, cols(h, HALF)],
                op0=ALU.mult,
                op1=ALU.mult,
                accum_out=part[h][:, t : t + 1],
            )

        def finish_gate(t):
            agree(1, t)
            nc.scalar.activation(
                out=gate[:, t : t + 1], in_=part[1][:, t : t + 1], func=ACT.Tanh, bias=part[0][:, t : t + 1]
            )

        def blend(t, pieces):
            width = N // pieces
            for i in range(pieces):
                nc.vector.scalar_tensor_tensor(
                    out=y_sb[t][:, cols(i, width)],
                    in0=b_sb[t][:, cols(i, width)],
                    scalar=gate[:, t : t + 1],
                    in1=a_sb[:, t, :] if pieces == 1 else a_view(i, t),
                    op0=ALU.mult,
                    op1=ALU.add,
                )
                nc.sync.dma_start(out=out[cols(t), cols(i, width)], in_=y_sb[t][:, cols(i, width)])

        for t in range(3):
            product_b(t)
        cast(nc.vector.tensor_copy, 0, 0)
        quantize(0, 0)
        cast(nc.scalar.copy, 0, 1)
        for t in range(3):
            offset_b(t)
        quantize(0, 1)
        product_wa(0, 0, first=True)
        product_b(3)
        offset_b(3)
        product_ws(0)
        product_wa(0, 1, last=True)
        product_ws(1, first=True)
        for j, tag in enumerate(("A11", "B2")):
            at_ps[j] = ps.tile([P, HALF], F32, name="at_ps%d" % j, tag=tag)
            turned_ws(j)
        bias_n_ps = ps.tile([P, 2, P], F32, name="bias_n_ps", tag="B1")
        for j in range(2):
            nc.tensor.transpose(bias_n_ps[:, j, :], bias_row[:, cols(2 + j)], ident[:])
        cast(nc.scalar.copy, 1, 0)
        offset_a(0, 0)
        quantize(1, 0)
        cast(nc.scalar.copy, 1, 1)
        nc.scalar.copy(out=bias_n[:], in_=bias_n_ps[:, :, 0])
        offset_a(0, 1)
        product_wa(1, 0)
        for j in range(2):
            turned_wa(j, 0)
        agree(0, 0)
        quantize(1, 1)
        product_wa(1, 1, last=True)
        for j in range(2):
            turned_wa(j, 1)
        turned["a"] = ps.tile([P, 2, HALF], F32, name="a_turned", tag="B0")
        for j in range(2):
            nc.scalar.activation(out=at_sb[j][:], in_=at_ps[j][:], func=ACT.Identity, bias=bias_n[:, j : j + 1])
            for t in range(2):
                nc.tensor.transpose(turned["a"][:, t, cols(j)], at_sb[j][:, cols(t)], ident[:])
        agree(0, 1)
        agree(0, 2)
        offset_a(1, 0)
        agree(0, 3)
        finish_gate(0)
        finish_gate(1)
        blend(0, 1)
        finish_gate(2)
        blend(1, 1)
        finish_gate(3)
        blend(2, 2)
        blend(3, 2)
